import numpy as np
import ml_dtypes


def mxq(x, axis, fmt="e4m3"):
    dtype, down = {"e4m3": (ml_dtypes.float8_e4m3fn, 7), "e5m2": (ml_dtypes.float8_e5m2, 14)}[fmt]
    v = np.moveaxis(np.asarray(x, np.float32).astype(ml_dtypes.bfloat16).astype(np.float64), axis, -1)
    blocks = v.reshape(v.shape[:-1] + (-1, 32))
    amax = np.abs(blocks).max(-1, keepdims=True)
    byte = np.maximum(np.where(amax > 0, np.frexp(amax)[1] - 1 + 127, 0) - down, 1)
    scale = np.exp2(byte - 127.0)
    codes = (blocks / scale).astype(np.float32).astype(dtype).astype(np.float64)
    return np.moveaxis((codes * scale).reshape(v.shape), -1, axis)


WIDE = False


def mx_kscale(k):
    if not WIDE:
        return np.ones(k)
    levels = np.array([10, -10, 5, -5, 0])
    if k % 512:
        return np.exp2(np.random.permutation(np.resize(levels, k // 32))).repeat(32)
    a = np.empty((k // 512, 16))
    for p in range(k // 512):
        a[p, :8] = np.random.permutation(np.resize(levels, 8))
        for g in range(8):
            far = levels[np.abs(levels - a[p, g]) >= 10]
            a[p, g + 8] = far[np.random.randint(len(far))]
    return np.exp2(a.ravel()).repeat(32)


def f64(x):
    return np.asarray(x).astype(np.float64)


def striped(idx):
    return np.tile(np.asarray(idx).reshape(-1, 16).T, (8, 1)).astype(np.uint16)


def unstriped(offs):
    return offs[:16].T.reshape(-1).astype(np.int64)


B, N, T, D, DV, NQ = 1, 512, 2048, 1536, 128, 128


def setup_inputs():
    n = np.random.standard_normal
    idx = np.random.permutation(T)[:B * N]
    s = mx_kscale(D)[:, None]
    u = np.ones(T)
    u[idx] = mx_kscale(B * N)
    r = np.random.uniform(0.5, 2.0, T)
    k = n((D, T)) / s
    v = n((DV, T)) / (u * r)
    return {
        "qT": (n((B, D, NQ)) * s * (0.80 / np.sqrt(D))).astype(np.float32),
        "kT": k.astype(np.float32),
        "vT": v.astype(np.float32),
        "vs": np.tile(u * r, (128, 1)).astype(np.float32),
        "offs": striped(idx),
    }


def reference(qT, kT, vT, vs, offs):
    idx = unstriped(offs)
    k = f64(kT)
    v = f64(vT)
    pick = lambda x: x[:, idx].reshape(x.shape[0], B, N).transpose(1, 0, 2)
    q = f64(qT)
    score = mxq(q, 1, "e4m3").transpose(0, 2, 1) @ mxq(pick(k), 1, "e4m3")
    m = score.max(-1, keepdims=True)
    p = np.exp(score - m)
    total = p.sum(-1, keepdims=True)
    w = p * pick(f64(vs))[:, :1, :]
    y = mxq(w, 2, "e4m3") @ mxq(pick(v).transpose(0, 2, 1), 1, "e4m3")
    y = y / total
    return y

@@ -1,0 +1,231 @@
+from contextlib import ExitStack
+
+import concourse.mybir as mybir
+from concourse.masks import make_identity
+
+P = 128
+D = 1536
+T = 2048
+N = 512
+NQ = 128
+DV = 128
+PACK = 4
+K_PASS = P * PACK
+PASSES = D // K_PASS
+S = N // PACK
+HALF = N // 2
+
+FLOPS = 2 * NQ * N * D + 2 * NQ * N * DV
+BYTES = 4 * (D * T + DV * T + T + D * NQ + NQ * DV) + 2 * P * (N // 16)
+
+F32 = mybir.dt.float32
+BF16 = mybir.dt.bfloat16
+U32 = mybir.dt.uint32
+U16 = mybir.dt.uint16
+U8 = mybir.dt.uint8
+FP8X4 = mybir.dt.float8_e4m3fn_x4
+Exp = mybir.ActivationFunctionType.Exp
+Copy = mybir.ActivationFunctionType.Copy
+mult = mybir.AluOpType.mult
+X = mybir.AxisListType.X
+
+
+def tile_attend_knn_kernel(tc, qT, kT, vT, vs, offs, out):
+    nc = tc.nc
+    with ExitStack() as ctx:
+        keep = ctx.enter_context(tc.tile_pool(name="keep", bufs=1))
+        psum = ctx.enter_context(tc.psum_pool(name="psum", bufs=1))
+
+        offsets = keep.tile([P, N // 16], U16, name="offsets")
+        nc.sync.dma_start(offsets[:], offs)
+
+        vs_pool = keep.tile([P, T], F32, name="vs_pool")
+        nc.vector.memset(vs_pool[:], 0.0)
+
+        k_rows = kT.rearrange("(g p j) w -> g p j w", p=P, j=PACK)
+        q_rows = qT.rearrange("b (g p j) w -> b g p j w", p=P, j=PACK)
+        k_pool = []
+        q_raw = []
+
+        def load_k(g, j):
+            tile = keep.tile([P, T], F32, name=f"k_pool_{g}_{j}")
+            nc.sync.dma_start(tile[:], k_rows[g, :, j, :])
+            k_pool.append(tile)
+
+        def load_q(g):
+            tile = keep.tile([P, PACK, NQ], F32, name=f"q_raw_{g}")
+            nc.sync.dma_start(tile[:], q_rows[0, g])
+            q_raw.append(tile)
+
+        for g in range(PASSES):
+            for j in range(PACK):
+                load_k(g, j)
+                if g == 0 and j == 0:
+                    nc.sync.dma_start(vs_pool[0:1, :], vs[0:1, :])
+        for g in range(PASSES):
+            load_q(g)
+        v_pool = keep.tile([P, T], F32, name="v_pool")
+        nc.sync.dma_start(v_pool[:], vT)
+
+        ident_f32 = keep.tile([P, P], F32, name="ident_f32")
+        make_identity(nc, ident_f32[:])
+        ident_bf16 = keep.tile([P, P], BF16, name="ident_bf16")
+        make_identity(nc, ident_bf16[:])
+        warm = keep.tile([P, 1], F32, name="warm")
+        nc.scalar.activation(warm[:], ident_f32[:, 0:1], Exp)
+
+        score = psum.tile([P, N], F32, name="score")
+        k_wide = [keep.tile([P, PACK, N], F32, name=f"k_wide_{g}") for g in range(PASSES - 1)]
+        k_grouped = []
+        k_codes = []
+        k_scales = []
+        q_grouped = []
+        q_codes = []
+        q_scales = []
+        for g in range(PASSES):
+            k_grouped.append(keep.tile([P, N, PACK], BF16, name=f"k_grouped_{g}", align_bytes=64))
+            k_codes.append(keep.tile([P, N], U32, name=f"k_codes_{g}", align_bytes=64))
+            k_scales.append(keep.tile([P, N], U8, name=f"k_scales_{g}", align_bytes=64))
+            q_grouped.append(keep.tile([P, NQ, PACK], BF16, name=f"q_grouped_{g}", align_bytes=64))
+            q_codes.append(keep.tile([P, NQ], U32, name=f"q_codes_{g}", align_bytes=64))
+            q_scales.append(keep.tile([P, NQ], U8, name=f"q_scales_{g}", align_bytes=64))
+
+        def gather_wide(g, j):
+            nc.vector.tensor_copy(k_wide[g][:, j, :], k_pool[g * PACK + j][:].indirect(offsets[:]))
+
+        def group_k(g):
+            nc.scalar.copy(k_grouped[g][:], k_wide[g][:].rearrange("p j i -> p i j"))
+
+        def gather_k(g, j, lo, hi):
+            nc.vector.tensor_copy(
+                k_grouped[g][:, lo:hi, j],
+                k_pool[g * PACK + j][:].indirect(offsets[:, lo // 16 : hi // 16]),
+            )
+
+        def quantize_k(g, lo, hi):
+            nc.vector.quantize_mx(
+                out=k_codes[g][:, lo:hi].bitcast(FP8X4),
+                scales=k_scales[g][:, lo:hi],
+                in_=k_grouped[g][:, lo:hi, :].rearrange("p i j -> p (i j)"),
+            )
+
+        def group_q(g):
+            nc.scalar.copy(q_grouped[g][:], q_raw[g][:].rearrange("p j q -> p q j"))
+
+        def quantize_q(g):
+            nc.vector.quantize_mx(
+                out=q_codes[g][:].bitcast(FP8X4),
+                scales=q_scales[g][:],
+                in_=q_grouped[g][:].rearrange("p q j -> p (q j)"),
+            )
+
+        def multiply(g):
+            nc.tensor.matmul_mx(
+                out=score[:],
+                lhsT=q_codes[g][:].bitcast(FP8X4),
+                lhsT_scale=q_scales[g][:],
+                rhs=k_codes[g][:].bitcast(FP8X4),
+                rhs_scale=k_scales[g][:],
+                start=(g == 0),
+                stop=(g == PASSES - 1),
+            )
+
+        for g in range(PASSES - 1):
+            for j in range(PACK):
+                gather_wide(g, j)
+            group_k(g)
+            quantize_k(g, 0, N)
+
+        vs_row = keep.tile([P, N], F32, name="vs_row")
+        nc.vector.tensor_copy(vs_row[:], vs_pool[:].indirect(offsets[:]))
+        vs_turned = psum.tile([P, PACK, P], F32, name="vs_turned")
+        for t in range(PACK):
+            nc.tensor.transpose(vs_turned[:, t, :], vs_row[:, t:N:PACK], ident_f32[:])
+        vs_slot = keep.tile([P, PACK], F32, name="vs_slot")
+        nc.vector.tensor_copy(vs_slot[:], vs_turned[:, :, 0])
+
+        for j in range(PACK - 1):
+            gather_k(2, j, 0, N)
+        gather_k(2, 3, 0, HALF)
+        gather_k(2, 3, HALF, N)
+        group_q(0)
+        quantize_q(0)
+        multiply(0)
+        quantize_k(2, 0, HALF)
+        quantize_k(2, HALF, N)
+        group_q(1)
+        quantize_q(1)
+        multiply(1)
+        nc.vector.tensor_copy(q_grouped[2][:], q_raw[2][:].rearrange("p j q -> p q j"))
+        quantize_q(2)
+        multiply(2)
+
+        neg_m = keep.tile([P, 1], F32, name="neg_m")
+        l_half = keep.tile([P, 2], F32, name="l_half")
+        l_sum = keep.tile([P, 1], F32, name="l_sum")
+        l_inv = keep.tile([P, 1], F32, name="l_inv")
+        prob = keep.tile([P, PACK, S], F32, name="prob")
+        nc.vector.reduce_max(neg_m[:], score[:], axis=X, negate=True)
+        for h in range(2):
+            nc.scalar.activation(
+                prob[:, 2 * h : 2 * h + 2, :],
+                score[:].rearrange("p (s t) -> p t s", t=PACK)[:, 2 * h : 2 * h + 2, :],
+                Exp,
+                bias=neg_m[:],
+                accum_out=l_half[:, h : h + 1],
+            )
+
+        v_slots = keep.tile([P, PACK, S], BF16, name="v_slots")
+        nc.vector.tensor_copy(v_slots[:].rearrange("p t s -> p s t"), v_pool[:].indirect(offsets[:]))
+
+        p_turned = psum.tile([P, PACK, NQ], F32, name="p_turned")
+        for t in range(PACK):
+            nc.tensor.transpose(p_turned[:, t, :], prob[:, t, :], ident_f32[:])
+        v_turned = psum.tile([P, PACK, DV], BF16, name="v_turned")
+        for t in range(PACK):
+            nc.tensor.transpose(v_turned[:, t, :], v_slots[:, t, :], ident_bf16[:])
+
+        w_grouped = keep.tile([P, NQ, PACK], BF16, name="w_grouped", align_bytes=64)
+        w_codes = keep.tile([P, NQ], U32, name="w_codes", align_bytes=64)
+        w_scales = keep.tile([P, NQ], U8, name="w_scales", align_bytes=64)
+        QH = NQ // 2
+        for h in range(2):
+            qs = slice(h * QH, (h + 1) * QH)
+            nc.vector.tensor_tensor(
+                w_grouped[:, qs, :],
+                p_turned[:, :, qs].rearrange("p t q -> p q t"),
+                vs_slot[:].unsqueeze(1).to_broadcast([P, QH, PACK]),
+                mult,
+            )
+        for h in range(2):
+            qs = slice(h * QH, (h + 1) * QH)
+            nc.vector.quantize_mx(
+                out=w_codes[:, qs].bitcast(FP8X4),
+                scales=w_scales[:, qs],
+                in_=w_grouped[:, qs, :].rearrange("p q t -> p (q t)"),
+            )
+        v_grouped = keep.tile([P, DV, PACK], BF16, name="v_grouped", align_bytes=64)
+        v_codes = keep.tile([P, DV], U32, name="v_codes", align_bytes=64)
+        v_scales = keep.tile([P, DV], U8, name="v_scales", align_bytes=64)
+        nc.scalar.copy(v_grouped[:], v_turned[:].rearrange("p t e -> p e t"))
+        nc.vector.quantize_mx(
+            out=v_codes[:].bitcast(FP8X4),
+            scales=v_scales[:],
+            in_=v_grouped[:].rearrange("p e t -> p (e t)"),
+        )
+        nc.vector.tensor_add(l_sum[:], l_half[:, 0:1], l_half[:, 1:2])
+        nc.vector.reciprocal(l_inv[:], l_sum[:])
+
+        y = psum.tile([P, DV], F32, name="y")
+        nc.tensor.matmul_mx(
+            out=y[:],
+            lhsT=w_codes[:].bitcast(FP8X4),
+            lhsT_scale=w_scales[:],
+            rhs=v_codes[:].bitcast(FP8X4),
+            rhs_scale=v_scales[:],
+            start=True,
+            stop=True,
+        )
+        result = keep.tile([P, DV], F32, name="result")
+        nc.scalar.activation(result[:], y[:], Copy, scale=l_inv[:])
+        nc.sync.dma_start(out[0], result[:])

@@ -25,7 +25,7 @@ U16 = mybir.dt.uint16
 U8 = mybir.dt.uint8
 FP8X4 = mybir.dt.float8_e4m3fn_x4
 Exp = mybir.ActivationFunctionType.Exp
-Copy = mybir.ActivationFunctionType.Copy
+Identity = mybir.ActivationFunctionType.Identity
 mult = mybir.AluOpType.mult
 X = mybir.AxisListType.X
 
@@ -69,12 +69,10 @@ def tile_attend_knn_kernel(tc, qT, kT, vT, vs, offs, out):
 
         ident_f32 = keep.tile([P, P], F32, name="ident_f32")
         make_identity(nc, ident_f32[:])
-        ident_bf16 = keep.tile([P, P], BF16, name="ident_bf16")
-        make_identity(nc, ident_bf16[:])
         warm = keep.tile([P, 1], F32, name="warm")
         nc.scalar.activation(warm[:], ident_f32[:, 0:1], Exp)
 
-        score = psum.tile([P, N], F32, name="score")
+        score = psum.tile([P, N], F32, name="score", tag="score_bank")
         k_wide = [keep.tile([P, PACK, N], F32, name=f"k_wide_{g}") for g in range(PASSES - 1)]
         k_grouped = []
         k_codes = []
@@ -110,7 +108,10 @@ def tile_attend_knn_kernel(tc, qT, kT, vT, vs, offs, out):
             )
 
         def group_q(g):
-            nc.scalar.copy(q_grouped[g][:], q_raw[g][:].rearrange("p j q -> p q j"))
+            nc.scalar.copy(
+                q_grouped[g][:].rearrange("p (c i) j -> p c j i", i=PACK),
+                q_raw[g][:].rearrange("p j (c i) -> p c j i", i=PACK),
+            )
 
         def quantize_q(g):
             nc.vector.quantize_mx(
@@ -156,7 +157,7 @@ def tile_attend_knn_kernel(tc, qT, kT, vT, vs, offs, out):
         group_q(1)
         quantize_q(1)
         multiply(1)
-        nc.vector.tensor_copy(q_grouped[2][:], q_raw[2][:].rearrange("p j q -> p q j"))
+        group_q(2)
         quantize_q(2)
         multiply(2)
 
@@ -175,15 +176,18 @@ def tile_attend_knn_kernel(tc, qT, kT, vT, vs, offs, out):
                 accum_out=l_half[:, h : h + 1],
             )
 
-        v_slots = keep.tile([P, PACK, S], BF16, name="v_slots")
-        nc.vector.tensor_copy(v_slots[:].rearrange("p t s -> p s t"), v_pool[:].indirect(offsets[:]))
+        nc.scalar.activation(l_sum[:], l_half[:, 0:1], Identity, bias=l_half[:, 1:2])
+        v_pairs = keep.tile([P, 2, S, 2], BF16, name="v_pairs")
+        nc.vector.tensor_copy(v_pairs[:].rearrange("p u s e -> p s u e"), v_pool[:].indirect(offsets[:]))
+        v_words = v_pairs[:].rearrange("p u s e -> p (u s e)").bitcast(F32)
 
         p_turned = psum.tile([P, PACK, NQ], F32, name="p_turned")
         for t in range(PACK):
             nc.tensor.transpose(p_turned[:, t, :], prob[:, t, :], ident_f32[:])
-        v_turned = psum.tile([P, PACK, DV], BF16, name="v_turned")
-        for t in range(PACK):
-            nc.tensor.transpose(v_turned[:, t, :], v_slots[:, t, :], ident_bf16[:])
+        v_turned = psum.tile([P, 2, DV], F32, name="v_turned", tag="score_bank")
+        for u in range(2):
+            nc.tensor.transpose(v_turned[:, u, :], v_words[:, u * S : (u + 1) * S], ident_f32[:])
+        nc.vector.reciprocal(l_inv[:], l_sum[:])
 
         w_grouped = keep.tile([P, NQ, PACK], BF16, name="w_grouped", align_bytes=64)
         w_codes = keep.tile([P, NQ], U32, name="w_codes", align_bytes=64)
@@ -207,14 +211,15 @@ def tile_attend_knn_kernel(tc, qT, kT, vT, vs, offs, out):
         v_grouped = keep.tile([P, DV, PACK], BF16, name="v_grouped", align_bytes=64)
         v_codes = keep.tile([P, DV], U32, name="v_codes", align_bytes=64)
         v_scales = keep.tile([P, DV], U8, name="v_scales", align_bytes=64)
-        nc.scalar.copy(v_grouped[:], v_turned[:].rearrange("p t e -> p e t"))
+        nc.scalar.copy(
+            v_grouped[:].rearrange("p e t -> p (e t)").bitcast(F32).rearrange("p (e u) -> p e u", u=2),
+            v_turned[:].rearrange("p u e -> p e u"),
+        )
         nc.vector.quantize_mx(
             out=v_codes[:].bitcast(FP8X4),
             scales=v_scales[:],
             in_=v_grouped[:].rearrange("p e t -> p (e t)"),
         )
-        nc.vector.tensor_add(l_sum[:], l_half[:, 0:1], l_half[:, 1:2])
-        nc.vector.reciprocal(l_inv[:], l_sum[:])
 
         y = psum.tile([P, DV], F32, name="y")
         nc.tensor.matmul_mx(
@@ -227,5 +232,5 @@ def tile_attend_knn_kernel(tc, qT, kT, vT, vs, offs, out):
             stop=True,
         )
         result = keep.tile([P, DV], F32, name="result")
-        nc.scalar.activation(result[:], y[:], Copy, scale=l_inv[:])
+        nc.vector.tensor_scalar(result[:], y[:], l_inv[:], None, mult)
         nc.sync.dma_start(out[0], result[:])

@@ -47,10 +47,10 @@ def tile_attend_knn_kernel(tc, qT, kT, vT, vs, offs, out):
         k_pool = []
         q_raw = []
 
-        def load_k(g, j):
-            tile = keep.tile([P, T], F32, name=f"k_pool_{g}_{j}")
-            nc.sync.dma_start(tile[:], k_rows[g, :, j, :])
-            k_pool.append(tile)
+        def load_k(g, j, count):
+            tile = keep.tile([P, count, T], F32, name=f"k_pool_{g}_{j}", tag=f"k_pool_{g}_{j}", align_bytes=64)
+            nc.sync.dma_start(tile[:], k_rows[g, :, j : j + count, :])
+            k_pool.extend(tile[:, c, :] for c in range(count))
 
         def load_q(g):
             tile = keep.tile([P, PACK, NQ], F32, name=f"q_raw_{g}")
@@ -58,10 +58,11 @@ def tile_attend_knn_kernel(tc, qT, kT, vT, vs, offs, out):
             q_raw.append(tile)
 
         for g in range(PASSES):
-            for j in range(PACK):
-                load_k(g, j)
-                if g == 0 and j == 0:
-                    nc.sync.dma_start(vs_pool[0:1, :], vs[0:1, :])
+            count = PACK >> g
+            for j in range(0, PACK, count):
+                load_k(g, j, count)
+            if g == 0:
+                nc.sync.dma_start(vs_pool[0:1, :], vs[0:1, :])
         for g in range(PASSES):
             load_q(g)
         v_pool = keep.tile([P, T], F32, name="v_pool")
@@ -74,6 +75,7 @@ def tile_attend_knn_kernel(tc, qT, kT, vT, vs, offs, out):
 
         score = psum.tile([P, N], F32, name="score", tag="score_bank")
         k_wide = [keep.tile([P, PACK, N], F32, name=f"k_wide_{g}") for g in range(PASSES - 1)]
+        code_tags = ["k_pool_1_0", "k_pool_2_1", "k_codes_2"]
         k_grouped = []
         k_codes = []
         k_scales = []
@@ -82,22 +84,25 @@ def tile_attend_knn_kernel(tc, qT, kT, vT, vs, offs, out):
         q_scales = []
         for g in range(PASSES):
             k_grouped.append(keep.tile([P, N, PACK], BF16, name=f"k_grouped_{g}", align_bytes=64))
-            k_codes.append(keep.tile([P, N], U32, name=f"k_codes_{g}", align_bytes=64))
+            k_codes.append(keep.tile([P, N], U32, name=f"k_codes_{g}", tag=code_tags[g], align_bytes=64))
             k_scales.append(keep.tile([P, N], U8, name=f"k_scales_{g}", align_bytes=64))
             q_grouped.append(keep.tile([P, NQ, PACK], BF16, name=f"q_grouped_{g}", align_bytes=64))
             q_codes.append(keep.tile([P, NQ], U32, name=f"q_codes_{g}", align_bytes=64))
             q_scales.append(keep.tile([P, NQ], U8, name=f"q_scales_{g}", align_bytes=64))
 
         def gather_wide(g, j):
-            nc.vector.tensor_copy(k_wide[g][:, j, :], k_pool[g * PACK + j][:].indirect(offsets[:]))
+            nc.vector.tensor_copy(k_wide[g][:, j, :], k_pool[g * PACK + j].indirect(offsets[:]))
 
         def group_k(g):
-            nc.scalar.copy(k_grouped[g][:], k_wide[g][:].rearrange("p j i -> p i j"))
+            nc.scalar.copy(
+                k_grouped[g][:].rearrange("p (c i) j -> p c j i", i=PACK),
+                k_wide[g][:].rearrange("p j (c i) -> p c j i", i=PACK),
+            )
 
         def gather_k(g, j, lo, hi):
             nc.vector.tensor_copy(
                 k_grouped[g][:, lo:hi, j],
-                k_pool[g * PACK + j][:].indirect(offsets[:, lo // 16 : hi // 16]),
+                k_pool[g * PACK + j].indirect(offsets[:, lo // 16 : hi // 16]),
             )
 
         def quantize_k(g, lo, hi):
@@ -134,8 +139,9 @@ def tile_attend_knn_kernel(tc, qT, kT, vT, vs, offs, out):
         for g in range(PASSES - 1):
             for j in range(PACK):
                 gather_wide(g, j)
+                if g == 1 and j == 1:
+                    quantize_k(0, 0, N)
             group_k(g)
-            quantize_k(g, 0, N)
 
         vs_row = keep.tile([P, N], F32, name="vs_row")
         nc.vector.tensor_copy(vs_row[:], vs_pool[:].indirect(offsets[:]))
@@ -143,10 +149,12 @@ def tile_attend_knn_kernel(tc, qT, kT, vT, vs, offs, out):
         for t in range(PACK):
             nc.tensor.transpose(vs_turned[:, t, :], vs_row[:, t:N:PACK], ident_f32[:])
         vs_slot = keep.tile([P, PACK], F32, name="vs_slot")
-        nc.vector.tensor_copy(vs_slot[:], vs_turned[:, :, 0])
+        nc.scalar.copy(vs_slot[:], vs_turned[:, :, 0])
 
         for j in range(PACK - 1):
             gather_k(2, j, 0, N)
+            if j == 1:
+                quantize_k(1, 0, N)
         gather_k(2, 3, 0, HALF)
         gather_k(2, 3, HALF, N)
         group_q(0)

@@ -47,10 +47,10 @@ def tile_attend_knn_kernel(tc, qT, kT, vT, vs, offs, out):
         k_pool = []
         q_raw = []
 
-        def load_k(g, j, count):
-            tile = keep.tile([P, count, T], F32, name=f"k_pool_{g}_{j}", tag=f"k_pool_{g}_{j}", align_bytes=64)
-            nc.sync.dma_start(tile[:], k_rows[g, :, j : j + count, :])
-            k_pool.extend(tile[:, c, :] for c in range(count))
+        def load_k(g, j):
+            tile = keep.tile([P, T], F32, name=f"k_pool_{g}_{j}", tag=f"k_pool_{g}_{j}", align_bytes=64)
+            nc.sync.dma_start(tile[:], k_rows[g, :, j, :])
+            k_pool.append(tile[:])
 
         def load_q(g):
             tile = keep.tile([P, PACK, NQ], F32, name=f"q_raw_{g}")
@@ -58,11 +58,10 @@ def tile_attend_knn_kernel(tc, qT, kT, vT, vs, offs, out):
             q_raw.append(tile)
 
         for g in range(PASSES):
-            count = PACK >> g
-            for j in range(0, PACK, count):
-                load_k(g, j, count)
-            if g == 0:
-                nc.sync.dma_start(vs_pool[0:1, :], vs[0:1, :])
+            for j in range(PACK):
+                load_k(g, j)
+                if g == 0 and j == 1:
+                    nc.sync.dma_start(vs_pool[0:1, :], vs[0:1, :])
         for g in range(PASSES):
             load_q(g)
         v_pool = keep.tile([P, T], F32, name="v_pool")
@@ -75,7 +74,7 @@ def tile_attend_knn_kernel(tc, qT, kT, vT, vs, offs, out):
 
         score = psum.tile([P, N], F32, name="score", tag="score_bank")
         k_wide = [keep.tile([P, PACK, N], F32, name=f"k_wide_{g}") for g in range(PASSES - 1)]
-        code_tags = ["k_pool_1_0", "k_pool_2_1", "k_codes_2"]
+        code_tags = ["k_pool_1_1", "k_pool_2_1", "k_codes_2"]
         k_grouped = []
         k_codes = []
         k_scales = []

@@ -13,7 +13,7 @@ PACK = 4
 K_PASS = P * PACK
 PASSES = D // K_PASS
 S = N // PACK
-HALF = N // 2
+RUN = T // P
 
 FLOPS = 2 * NQ * N * D + 2 * NQ * N * DV
 BYTES = 4 * (D * T + DV * T + T + D * NQ + NQ * DV) + 2 * P * (N // 16)
@@ -37,10 +37,7 @@ def tile_attend_knn_kernel(tc, qT, kT, vT, vs, offs, out):
         psum = ctx.enter_context(tc.psum_pool(name="psum", bufs=1))
 
         offsets = keep.tile([P, N // 16], U16, name="offsets")
-        nc.sync.dma_start(offsets[:], offs)
-
-        vs_pool = keep.tile([P, T], F32, name="vs_pool")
-        nc.vector.memset(vs_pool[:], 0.0)
+        vs_runs = keep.tile([P, RUN], F32, name="vs_runs")
 
         k_rows = kT.rearrange("(g p j) w -> g p j w", p=P, j=PACK)
         q_rows = qT.rearrange("b (g p j) w -> b g p j w", p=P, j=PACK)
@@ -53,15 +50,16 @@ def tile_attend_knn_kernel(tc, qT, kT, vT, vs, offs, out):
             k_pool.append(tile[:])
 
         def load_q(g):
-            tile = keep.tile([P, PACK, NQ], F32, name=f"q_raw_{g}")
+            tile = keep.tile([P, PACK, NQ], F32, name=f"q_raw_{g}", tag=f"q_raw_{g}", align_bytes=64)
             nc.sync.dma_start(tile[:], q_rows[0, g])
             q_raw.append(tile)
 
         for g in range(PASSES):
             for j in range(PACK):
                 load_k(g, j)
-                if g == 0 and j == 1:
-                    nc.sync.dma_start(vs_pool[0:1, :], vs[0:1, :])
+                if g == 0 and j == 0:
+                    nc.sync.dma_start(offsets[:], offs)
+                    nc.sync.dma_start(vs_runs[:], vs[0].rearrange("(p c) -> p c", c=RUN))
         for g in range(PASSES):
             load_q(g)
         v_pool = keep.tile([P, T], F32, name="v_pool")
@@ -72,9 +70,20 @@ def tile_attend_knn_kernel(tc, qT, kT, vT, vs, offs, out):
         warm = keep.tile([P, 1], F32, name="warm")
         nc.scalar.activation(warm[:], ident_f32[:, 0:1], Exp)
 
+        vs_pool = keep.tile([P, T], F32, name="vs_pool")
+        vs_by_run = vs_pool[:].rearrange("p (m c) -> p m c", c=RUN)
+        for b in range(RUN // PACK):
+            spread = psum.tile([P, PACK, P], F32, name=f"vs_spread_{b}")
+            for c in range(PACK):
+                column = PACK * b + c
+                nc.tensor.transpose(
+                    spread[:, c, :], vs_runs[:, column : column + 1].to_broadcast([P, P]), ident_f32[:]
+                )
+            nc.scalar.copy(vs_by_run[:, :, PACK * b : PACK * (b + 1)], spread[:].rearrange("p c m -> p m c"))
+
         score = psum.tile([P, N], F32, name="score", tag="score_bank")
         k_wide = [keep.tile([P, PACK, N], F32, name=f"k_wide_{g}") for g in range(PASSES - 1)]
-        code_tags = ["k_pool_1_1", "k_pool_2_1", "k_codes_2"]
+        code_tags = ["k_pool_1_1", "k_pool_2_1", "q_raw_1"]
         k_grouped = []
         k_codes = []
         k_scales = []
@@ -150,20 +159,17 @@ def tile_attend_knn_kernel(tc, qT, kT, vT, vs, offs, out):
         vs_slot = keep.tile([P, PACK], F32, name="vs_slot")
         nc.scalar.copy(vs_slot[:], vs_turned[:, :, 0])
 
-        for j in range(PACK - 1):
+        for j in range(PACK):
             gather_k(2, j, 0, N)
             if j == 1:
                 quantize_k(1, 0, N)
-        gather_k(2, 3, 0, HALF)
-        gather_k(2, 3, HALF, N)
         group_q(0)
         quantize_q(0)
         multiply(0)
-        quantize_k(2, 0, HALF)
-        quantize_k(2, HALF, N)
         group_q(1)
         quantize_q(1)
         multiply(1)
+        quantize_k(2, 0, N)
         group_q(2)
         quantize_q(2)
         multiply(2)

@@ -44,22 +44,23 @@ def tile_attend_knn_kernel(tc, qT, kT, vT, vs, offs, out):
         k_pool = []
         q_raw = []
 
-        def load_k(g, j):
-            tile = keep.tile([P, T], F32, name=f"k_pool_{g}_{j}", tag=f"k_pool_{g}_{j}", align_bytes=64)
-            nc.sync.dma_start(tile[:], k_rows[g, :, j, :])
-            k_pool.append(tile[:])
+        def load_k(g, j, count):
+            tile = keep.tile([P, count, T], F32, name=f"k_pool_{g}_{j}", tag=f"k_pool_{g}_{j}", align_bytes=64)
+            nc.sync.dma_start(tile[:], k_rows[g, :, j : j + count, :])
+            k_pool.extend(tile[:, c, :] for c in range(count))
 
         def load_q(g):
             tile = keep.tile([P, PACK, NQ], F32, name=f"q_raw_{g}", tag=f"q_raw_{g}", align_bytes=64)
             nc.sync.dma_start(tile[:], q_rows[0, g])
             q_raw.append(tile)
 
-        for g in range(PASSES):
-            for j in range(PACK):
-                load_k(g, j)
-                if g == 0 and j == 0:
-                    nc.sync.dma_start(offsets[:], offs)
-                    nc.sync.dma_start(vs_runs[:], vs[0].rearrange("(p c) -> p c", c=RUN))
+        load_k(0, 0, 2)
+        nc.sync.dma_start(offsets[:], offs)
+        nc.sync.dma_start(vs_runs[:], vs[0].rearrange("(p c) -> p c", c=RUN))
+        load_k(0, 2, 2)
+        load_k(1, 0, 2)
+        for plane in range(6, PASSES * PACK):
+            load_k(plane // PACK, plane % PACK, 1)
         for g in range(PASSES):
             load_q(g)
         v_pool = keep.tile([P, T], F32, name="v_pool")
@@ -83,7 +84,7 @@ def tile_attend_knn_kernel(tc, qT, kT, vT, vs, offs, out):
 
         score = psum.tile([P, N], F32, name="score", tag="score_bank")
         k_wide = [keep.tile([P, PACK, N], F32, name=f"k_wide_{g}") for g in range(PASSES - 1)]
-        code_tags = ["k_pool_1_1", "k_pool_2_1", "q_raw_1"]
+        code_tags = ["k_pool_1_0", "k_pool_2_1", "q_raw_1"]
         k_grouped = []
         k_codes = []
         k_scales = []

@@ -56,11 +56,12 @@ def tile_attend_knn_kernel(tc, qT, kT, vT, vs, offs, out):
 
         load_k(0, 0, 2)
         nc.sync.dma_start(offsets[:], offs)
-        nc.sync.dma_start(vs_runs[:], vs[0].rearrange("(p c) -> p c", c=RUN))
+        nc.scalar.dma_start(vs_runs[:], vs[0].rearrange("(p c) -> p c", c=RUN))
         load_k(0, 2, 2)
         load_k(1, 0, 2)
-        for plane in range(6, PASSES * PACK):
-            load_k(plane // PACK, plane % PACK, 1)
+        load_k(1, 2, 2)
+        for j in range(PACK):
+            load_k(2, j, 1)
         for g in range(PASSES):
             load_q(g)
         v_pool = keep.tile([P, T], F32, name="v_pool")
@@ -83,7 +84,8 @@ def tile_attend_knn_kernel(tc, qT, kT, vT, vs, offs, out):
             nc.scalar.copy(vs_by_run[:, :, PACK * b : PACK * (b + 1)], spread[:].rearrange("p c m -> p m c"))
 
         score = psum.tile([P, N], F32, name="score", tag="score_bank")
-        k_wide = [keep.tile([P, PACK, N], F32, name=f"k_wide_{g}") for g in range(PASSES - 1)]
+        wide_planes = [PACK, PACK, 2]
+        k_wide = [keep.tile([P, wide_planes[g], N], F32, name=f"k_wide_{g}") for g in range(PASSES)]
         code_tags = ["k_pool_1_0", "k_pool_2_1", "q_raw_1"]
         k_grouped = []
         k_codes = []
@@ -104,7 +106,7 @@ def tile_attend_knn_kernel(tc, qT, kT, vT, vs, offs, out):
 
         def group_k(g):
             nc.scalar.copy(
-                k_grouped[g][:].rearrange("p (c i) j -> p c j i", i=PACK),
+                k_grouped[g][:, :, 0 : wide_planes[g]].rearrange("p (c i) j -> p c j i", i=PACK),
                 k_wide[g][:].rearrange("p j (c i) -> p c j i", i=PACK),
             )
 
@@ -145,12 +147,6 @@ def tile_attend_knn_kernel(tc, qT, kT, vT, vs, offs, out):
                 stop=(g == PASSES - 1),
             )
 
-        for g in range(PASSES - 1):
-            for j in range(PACK):
-                gather_wide(g, j)
-                if g == 1 and j == 1:
-                    quantize_k(0, 0, N)
-            group_k(g)
 
         vs_row = keep.tile([P, N], F32, name="vs_row")
         nc.vector.tensor_copy(vs_row[:], vs_pool[:].indirect(offsets[:]))
@@ -160,10 +156,14 @@ def tile_attend_knn_kernel(tc, qT, kT, vT, vs, offs, out):
         vs_slot = keep.tile([P, PACK], F32, name="vs_slot")
         nc.scalar.copy(vs_slot[:], vs_turned[:, :, 0])
 
-        for j in range(PACK):
-            gather_k(2, j, 0, N)
-            if j == 1:
-                quantize_k(1, 0, N)
+        for g in range(PASSES):
+            for j in range(wide_planes[g]):
+                gather_wide(g, j)
+                if g > 0 and j == 1:
+                    quantize_k(g - 1, 0, N)
+            group_k(g)
+            for j in range(wide_planes[g], PACK):
+                gather_k(g, j, 0, N)
         group_q(0)
         quantize_q(0)
         multiply(0)

@@ -69,8 +69,6 @@ def tile_attend_knn_kernel(tc, qT, kT, vT, vs, offs, out):
 
         ident_f32 = keep.tile([P, P], F32, name="ident_f32")
         make_identity(nc, ident_f32[:])
-        warm = keep.tile([P, 1], F32, name="warm")
-        nc.scalar.activation(warm[:], ident_f32[:, 0:1], Exp)
 
         vs_pool = keep.tile([P, T], F32, name="vs_pool")
         vs_by_run = vs_pool[:].rearrange("p (m c) -> p m c", c=RUN)

@@ -84,7 +84,11 @@ def tile_attend_knn_kernel(tc, qT, kT, vT, vs, offs, out):
         score = psum.tile([P, N], F32, name="score", tag="score_bank")
         wide_planes = [PACK, PACK, 2]
         k_wide = [keep.tile([P, wide_planes[g], N], F32, name=f"k_wide_{g}") for g in range(PASSES)]
-        code_tags = ["k_pool_1_0", "k_pool_2_1", "q_raw_1"]
+        code_tags = ["k_pool_1_0", "k_pool_2_1"]
+        NH = N // 2
+        last_codes = [
+            keep.tile([P, NH], U32, name=f"last_codes_{h}", tag=f"q_raw_{h}", align_bytes=64) for h in range(2)
+        ]
         k_grouped = []
         k_codes = []
         k_scales = []
@@ -93,7 +97,8 @@ def tile_attend_knn_kernel(tc, qT, kT, vT, vs, offs, out):
         q_scales = []
         for g in range(PASSES):
             k_grouped.append(keep.tile([P, N, PACK], BF16, name=f"k_grouped_{g}", align_bytes=64))
-            k_codes.append(keep.tile([P, N], U32, name=f"k_codes_{g}", tag=code_tags[g], align_bytes=64))
+            if g < PASSES - 1:
+                k_codes.append(keep.tile([P, N], U32, name=f"k_codes_{g}", tag=code_tags[g], align_bytes=64))
             k_scales.append(keep.tile([P, N], U8, name=f"k_scales_{g}", align_bytes=64))
             q_grouped.append(keep.tile([P, NQ, PACK], BF16, name=f"q_grouped_{g}", align_bytes=64))
             q_codes.append(keep.tile([P, NQ], U32, name=f"q_codes_{g}", align_bytes=64))
@@ -121,6 +126,24 @@ def tile_attend_knn_kernel(tc, qT, kT, vT, vs, offs, out):
                 in_=k_grouped[g][:, lo:hi, :].rearrange("p i j -> p (i j)"),
             )
 
+        def quantize_last(h):
+            nc.vector.quantize_mx(
+                out=last_codes[h][:].bitcast(FP8X4),
+                scales=k_scales[2][:, h * NH : (h + 1) * NH],
+                in_=k_grouped[2][:, h * NH : (h + 1) * NH, :].rearrange("p i j -> p (i j)"),
+            )
+
+        def multiply_last(h):
+            nc.tensor.matmul_mx(
+                out=score[:, h * NH : (h + 1) * NH],
+                lhsT=q_codes[2][:].bitcast(FP8X4),
+                lhsT_scale=q_scales[2][:],
+                rhs=last_codes[h][:].bitcast(FP8X4),
+                rhs_scale=k_scales[2][:, h * NH : (h + 1) * NH],
+                start=False,
+                stop=(h == 1),
+            )
+
         def group_q(g):
             nc.scalar.copy(
                 q_grouped[g][:].rearrange("p (c i) j -> p c j i", i=PACK),
@@ -142,7 +165,7 @@ def tile_attend_knn_kernel(tc, qT, kT, vT, vs, offs, out):
                 rhs=k_codes[g][:].bitcast(FP8X4),
                 rhs_scale=k_scales[g][:],
                 start=(g == 0),
-                stop=(g == PASSES - 1),
+                stop=False,
             )
 
 
@@ -165,30 +188,29 @@ def tile_attend_knn_kernel(tc, qT, kT, vT, vs, offs, out):
         group_q(0)
         quantize_q(0)
         multiply(0)
+        quantize_last(0)
         group_q(1)
         quantize_q(1)
         multiply(1)
-        quantize_k(2, 0, N)
+        quantize_last(1)
         group_q(2)
         quantize_q(2)
-        multiply(2)
+        multiply_last(0)
+        multiply_last(1)
 
         neg_m = keep.tile([P, 1], F32, name="neg_m")
-        l_half = keep.tile([P, 2], F32, name="l_half")
+        l_part = keep.tile([P, PACK], F32, name="l_part")
+        l_copy = keep.tile([P, PACK], F32, name="l_copy")
         l_sum = keep.tile([P, 1], F32, name="l_sum")
         l_inv = keep.tile([P, 1], F32, name="l_inv")
         prob = keep.tile([P, PACK, S], F32, name="prob")
         nc.vector.reduce_max(neg_m[:], score[:], axis=X, negate=True)
-        for h in range(2):
+        for t in range(PACK):
             nc.scalar.activation(
-                prob[:, 2 * h : 2 * h + 2, :],
-                score[:].rearrange("p (s t) -> p t s", t=PACK)[:, 2 * h : 2 * h + 2, :],
-                Exp,
-                bias=neg_m[:],
-                accum_out=l_half[:, h : h + 1],
+                prob[:, t, :], score[:, t:N:PACK], Exp, bias=neg_m[:], accum_out=l_part[:, t : t + 1]
             )
 
-        nc.scalar.activation(l_sum[:], l_half[:, 0:1], Identity, bias=l_half[:, 1:2])
+        nc.scalar.activation(l_copy[:], l_part[:], Identity, accum_out=l_sum[:])
         v_pairs = keep.tile([P, 2, S, 2], BF16, name="v_pairs")
         nc.vector.tensor_copy(v_pairs[:].rearrange("p u s e -> p s u e"), v_pool[:].indirect(offsets[:]))
         v_words = v_pairs[:].rearrange("p u s e -> p (u s e)").bitcast(F32)
@@ -223,15 +245,16 @@ def tile_attend_knn_kernel(tc, qT, kT, vT, vs, offs, out):
         v_grouped = keep.tile([P, DV, PACK], BF16, name="v_grouped", align_bytes=64)
         v_codes = keep.tile([P, DV], U32, name="v_codes", align_bytes=64)
         v_scales = keep.tile([P, DV], U8, name="v_scales", align_bytes=64)
-        nc.scalar.copy(
-            v_grouped[:].rearrange("p e t -> p (e t)").bitcast(F32).rearrange("p (e u) -> p e u", u=2),
-            v_turned[:].rearrange("p u e -> p e u"),
-        )
-        nc.vector.quantize_mx(
-            out=v_codes[:].bitcast(FP8X4),
-            scales=v_scales[:],
-            in_=v_grouped[:].rearrange("p e t -> p (e t)"),
-        )
+        v_grouped_words = v_grouped[:].rearrange("p e t -> p (e t)").bitcast(F32).rearrange("p (e u) -> p e u", u=2)
+        EH = DV // 2
+        for h in range(2):
+            es = slice(h * EH, (h + 1) * EH)
+            nc.scalar.copy(v_grouped_words[:, es, :], v_turned[:, :, es].rearrange("p u e -> p e u"))
+            nc.vector.quantize_mx(
+                out=v_codes[:, es].bitcast(FP8X4),
+                scales=v_scales[:, es],
+                in_=v_grouped[:, es, :].rearrange("p e t -> p (e t)"),
+            )
 
         y = psum.tile([P, DV], F32, name="y")
         nc.tensor.matmul_mx(

@@ -73,7 +73,7 @@ def tile_attend_knn_kernel(tc, qT, kT, vT, vs, offs, out):
         vs_pool = keep.tile([P, T], F32, name="vs_pool")
         vs_by_run = vs_pool[:].rearrange("p (m c) -> p m c", c=RUN)
         for b in range(RUN // PACK):
-            spread = psum.tile([P, PACK, P], F32, name=f"vs_spread_{b}")
+            spread = psum.tile([P, PACK, P], F32, name=f"vs_spread_{b}", tag=f"vs_spread_{b}")
             for c in range(PACK):
                 column = PACK * b + c
                 nc.tensor.transpose(
@@ -82,8 +82,7 @@ def tile_attend_knn_kernel(tc, qT, kT, vT, vs, offs, out):
             nc.scalar.copy(vs_by_run[:, :, PACK * b : PACK * (b + 1)], spread[:].rearrange("p c m -> p m c"))
 
         score = psum.tile([P, N], F32, name="score", tag="score_bank")
-        wide_planes = [PACK, PACK, 2]
-        k_wide = [keep.tile([P, wide_planes[g], N], F32, name=f"k_wide_{g}") for g in range(PASSES)]
+        k_wide = [keep.tile([P, PACK, N], F32, name=f"k_wide_{g}") for g in range(PASSES - 1)]
         code_tags = ["k_pool_1_0", "k_pool_2_1"]
         NH = N // 2
         last_codes = [
@@ -109,7 +108,7 @@ def tile_attend_knn_kernel(tc, qT, kT, vT, vs, offs, out):
 
         def group_k(g):
             nc.scalar.copy(
-                k_grouped[g][:, :, 0 : wide_planes[g]].rearrange("p (c i) j -> p c j i", i=PACK),
+                k_grouped[g][:].rearrange("p (c i) j -> p c j i", i=PACK),
                 k_wide[g][:].rearrange("p j (c i) -> p c j i", i=PACK),
             )
 
@@ -178,13 +177,15 @@ def tile_attend_knn_kernel(tc, qT, kT, vT, vs, offs, out):
         nc.scalar.copy(vs_slot[:], vs_turned[:, :, 0])
 
         for g in range(PASSES):
-            for j in range(wide_planes[g]):
-                gather_wide(g, j)
+            for j in range(PACK):
+                if g < PASSES - 1:
+                    gather_wide(g, j)
+                else:
+                    gather_k(g, j, 0, N)
                 if g > 0 and j == 1:
                     quantize_k(g - 1, 0, N)
-            group_k(g)
-            for j in range(wide_planes[g], PACK):
-                gather_k(g, j, 0, N)
+            if g < PASSES - 1:
+                group_k(g)
         group_q(0)
         quantize_q(0)
         multiply(0)
@@ -256,16 +257,18 @@ def tile_attend_knn_kernel(tc, qT, kT, vT, vs, offs, out):
                 in_=v_grouped[:, es, :].rearrange("p e t -> p (e t)"),
             )
 
-        y = psum.tile([P, DV], F32, name="y")
-        nc.tensor.matmul_mx(
-            out=y[:],
-            lhsT=w_codes[:].bitcast(FP8X4),
-            lhsT_scale=w_scales[:],
-            rhs=v_codes[:].bitcast(FP8X4),
-            rhs_scale=v_scales[:],
-            start=True,
-            stop=True,
-        )
-        result = keep.tile([P, DV], F32, name="result")
-        nc.vector.tensor_scalar(result[:], y[:], l_inv[:], None, mult)
-        nc.sync.dma_start(out[0], result[:])
+        for h in range(2):
+            es = slice(h * EH, (h + 1) * EH)
+            y = psum.tile([P, EH], F32, name=f"y_{h}", tag=f"vs_spread_{h}")
+            nc.tensor.matmul_mx(
+                out=y[:],
+                lhsT=w_codes[:].bitcast(FP8X4),
+                lhsT_scale=w_scales[:],
+                rhs=v_codes[:, es].bitcast(FP8X4),
+                rhs_scale=v_scales[:, es],
+                start=True,
+                stop=True,
+            )
+            result = keep.tile([P, EH], F32, name=f"result_{h}")
+            nc.vector.tensor_scalar(result[:], y[:], l_inv[:], None, mult)
+            nc.sync.dma_start(out[0, :, es], result[:])

@@ -243,32 +243,32 @@ def tile_attend_knn_kernel(tc, qT, kT, vT, vs, offs, out):
                 scales=w_scales[:, qs],
                 in_=w_grouped[:, qs, :].rearrange("p q t -> p (q t)"),
             )
-        v_grouped = keep.tile([P, DV, PACK], BF16, name="v_grouped", align_bytes=64)
         v_codes = keep.tile([P, DV], U32, name="v_codes", align_bytes=64)
         v_scales = keep.tile([P, DV], U8, name="v_scales", align_bytes=64)
-        v_grouped_words = v_grouped[:].rearrange("p e t -> p (e t)").bitcast(F32).rearrange("p (e u) -> p e u", u=2)
         EH = DV // 2
         for h in range(2):
             es = slice(h * EH, (h + 1) * EH)
-            nc.scalar.copy(v_grouped_words[:, es, :], v_turned[:, :, es].rearrange("p u e -> p e u"))
+            v_grouped = keep.tile([P, EH * PACK], BF16, name=f"v_grouped_{h}", align_bytes=64)
+            nc.scalar.copy(
+                v_grouped[:].bitcast(F32).rearrange("p (e u) -> p e u", u=2),
+                v_turned[:, :, es].rearrange("p u e -> p e u"),
+            )
             nc.vector.quantize_mx(
                 out=v_codes[:, es].bitcast(FP8X4),
                 scales=v_scales[:, es],
-                in_=v_grouped[:, es, :].rearrange("p e t -> p (e t)"),
+                in_=v_grouped[:],
             )
 
-        for h in range(2):
-            es = slice(h * EH, (h + 1) * EH)
-            y = psum.tile([P, EH], F32, name=f"y_{h}", tag=f"vs_spread_{h}")
-            nc.tensor.matmul_mx(
-                out=y[:],
-                lhsT=w_codes[:].bitcast(FP8X4),
-                lhsT_scale=w_scales[:],
-                rhs=v_codes[:, es].bitcast(FP8X4),
-                rhs_scale=v_scales[:, es],
-                start=True,
-                stop=True,
-            )
-            result = keep.tile([P, EH], F32, name=f"result_{h}")
-            nc.vector.tensor_scalar(result[:], y[:], l_inv[:], None, mult)
-            nc.sync.dma_start(out[0, :, es], result[:])
+        y = psum.tile([P, DV], F32, name="y")
+        nc.tensor.matmul_mx(
+            out=y[:],
+            lhsT=w_codes[:].bitcast(FP8X4),
+            lhsT_scale=w_scales[:],
+            rhs=v_codes[:].bitcast(FP8X4),
+            rhs_scale=v_scales[:],
+            start=True,
+            stop=True,
+        )
+        result = keep.tile([P, DV], F32, name="result")
+        nc.vector.tensor_scalar(result[:], y[:], l_inv[:], None, mult)
+        nc.sync.dma_start(out[0], result[:])

@@ -88,6 +88,8 @@ def tile_attend_knn_kernel(tc, qT, kT, vT, vs, offs, out):
         last_codes = [
             keep.tile([P, NH], U32, name=f"last_codes_{h}", tag=f"q_raw_{h}", align_bytes=64) for h in range(2)
         ]
+        last_wide = keep.tile([P, 2, N], F32, name="last_wide")
+        last_grouped = [keep.tile([P, NH, PACK], BF16, name=f"last_grouped_{h}", align_bytes=64) for h in range(2)]
         k_grouped = []
         k_codes = []
         k_scales = []
@@ -95,7 +97,8 @@ def tile_attend_knn_kernel(tc, qT, kT, vT, vs, offs, out):
         q_codes = []
         q_scales = []
         for g in range(PASSES):
-            k_grouped.append(keep.tile([P, N, PACK], BF16, name=f"k_grouped_{g}", align_bytes=64))
+            if g < PASSES - 1:
+                k_grouped.append(keep.tile([P, N, PACK], BF16, name=f"k_grouped_{g}", align_bytes=64))
             if g < PASSES - 1:
                 k_codes.append(keep.tile([P, N], U32, name=f"k_codes_{g}", tag=code_tags[g], align_bytes=64))
             k_scales.append(keep.tile([P, N], U8, name=f"k_scales_{g}", align_bytes=64))
@@ -112,10 +115,16 @@ def tile_attend_knn_kernel(tc, qT, kT, vT, vs, offs, out):
                 k_wide[g][:].rearrange("p j (c i) -> p c j i", i=PACK),
             )
 
-        def gather_k(g, j, lo, hi):
+        def group_last(h):
+            nc.scalar.copy(
+                last_grouped[h][:, :, 0:2].rearrange("p (c i) j -> p c j i", i=PACK),
+                last_wide[:, :, h * NH : (h + 1) * NH].rearrange("p j (c i) -> p c j i", i=PACK),
+            )
+
+        def gather_last(j, h):
             nc.vector.tensor_copy(
-                k_grouped[g][:, lo:hi, j],
-                k_pool[g * PACK + j].indirect(offsets[:, lo // 16 : hi // 16]),
+                last_grouped[h][:, :, j],
+                k_pool[2 * PACK + j].indirect(offsets[:, h * NH // 16 : (h + 1) * NH // 16]),
             )
 
         def quantize_k(g, lo, hi):
@@ -129,7 +138,7 @@ def tile_attend_knn_kernel(tc, qT, kT, vT, vs, offs, out):
             nc.vector.quantize_mx(
                 out=last_codes[h][:].bitcast(FP8X4),
                 scales=k_scales[2][:, h * NH : (h + 1) * NH],
-                in_=k_grouped[2][:, h * NH : (h + 1) * NH, :].rearrange("p i j -> p (i j)"),
+                in_=last_grouped[h][:].rearrange("p i j -> p (i j)"),
             )
 
         def multiply_last(h):
@@ -176,16 +185,20 @@ def tile_attend_knn_kernel(tc, qT, kT, vT, vs, offs, out):
         vs_slot = keep.tile([P, PACK], F32, name="vs_slot")
         nc.scalar.copy(vs_slot[:], vs_turned[:, :, 0])
 
-        for g in range(PASSES):
+        for g in range(PASSES - 1):
             for j in range(PACK):
-                if g < PASSES - 1:
-                    gather_wide(g, j)
-                else:
-                    gather_k(g, j, 0, N)
+                gather_wide(g, j)
                 if g > 0 and j == 1:
                     quantize_k(g - 1, 0, N)
-            if g < PASSES - 1:
-                group_k(g)
+            group_k(g)
+        for j in range(2):
+            nc.vector.tensor_copy(last_wide[:, j, :], k_pool[2 * PACK + j].indirect(offsets[:]))
+        quantize_k(1, 0, N)
+        for h in range(2):
+            group_last(h)
+        for j in range(2, PACK):
+            for h in range(2):
+                gather_last(j, h)
         group_q(0)
         quantize_q(0)
         multiply(0)

@@ -36,8 +36,8 @@ def tile_attend_knn_kernel(tc, qT, kT, vT, vs, offs, out):
         keep = ctx.enter_context(tc.tile_pool(name="keep", bufs=1))
         psum = ctx.enter_context(tc.psum_pool(name="psum", bufs=1))
 
-        offsets = keep.tile([P, N // 16], U16, name="offsets")
-        vs_runs = keep.tile([P, RUN], F32, name="vs_runs")
+        offsets = keep.tile([P, N // 16], U16, name="offsets", align_bytes=256)
+        vs_runs = keep.tile([P, RUN], F32, name="vs_runs", align_bytes=256)
 
         k_rows = kT.rearrange("(g p j) w -> g p j w", p=P, j=PACK)
         q_rows = qT.rearrange("b (g p j) w -> b g p j w", p=P, j=PACK)
@@ -45,12 +45,12 @@ def tile_attend_knn_kernel(tc, qT, kT, vT, vs, offs, out):
         q_raw = []
 
         def load_k(g, j, count):
-            tile = keep.tile([P, count, T], F32, name=f"k_pool_{g}_{j}", tag=f"k_pool_{g}_{j}", align_bytes=64)
+            tile = keep.tile([P, count, T], F32, name=f"k_pool_{g}_{j}", tag=f"k_pool_{g}_{j}", align_bytes=256)
             nc.sync.dma_start(tile[:], k_rows[g, :, j : j + count, :])
             k_pool.extend(tile[:, c, :] for c in range(count))
 
         def load_q(g):
-            tile = keep.tile([P, PACK, NQ], F32, name=f"q_raw_{g}", tag=f"q_raw_{g}", align_bytes=64)
+            tile = keep.tile([P, PACK, NQ], F32, name=f"q_raw_{g}", tag=f"q_raw_{g}", align_bytes=256)
             nc.sync.dma_start(tile[:], q_rows[0, g])
             q_raw.append(tile)
 
@@ -64,7 +64,7 @@ def tile_attend_knn_kernel(tc, qT, kT, vT, vs, offs, out):
             load_k(2, j, 1)
         for g in range(PASSES):
             load_q(g)
-        v_pool = keep.tile([P, T], F32, name="v_pool")
+        v_pool = keep.tile([P, T], F32, name="v_pool", align_bytes=256)
         nc.sync.dma_start(v_pool[:], vT)
 
         ident_f32 = keep.tile([P, P], F32, name="ident_f32")
@@ -86,10 +86,10 @@ def tile_attend_knn_kernel(tc, qT, kT, vT, vs, offs, out):
         code_tags = ["k_pool_1_0", "k_pool_2_1"]
         NH = N // 2
         last_codes = [
-            keep.tile([P, NH], U32, name=f"last_codes_{h}", tag=f"q_raw_{h}", align_bytes=64) for h in range(2)
+            keep.tile([P, NH], U32, name=f"last_codes_{h}", tag=f"q_raw_{h}", align_bytes=256) for h in range(2)
         ]
         last_wide = keep.tile([P, 2, N], F32, name="last_wide")
-        last_grouped = [keep.tile([P, NH, PACK], BF16, name=f"last_grouped_{h}", align_bytes=64) for h in range(2)]
+        last_grouped = [keep.tile([P, NH, PACK], BF16, name=f"last_grouped_{h}", align_bytes=256) for h in range(2)]
         k_grouped = []
         k_codes = []
         k_scales = []
@@ -98,13 +98,13 @@ def tile_attend_knn_kernel(tc, qT, kT, vT, vs, offs, out):
         q_scales = []
         for g in range(PASSES):
             if g < PASSES - 1:
-                k_grouped.append(keep.tile([P, N, PACK], BF16, name=f"k_grouped_{g}", align_bytes=64))
+                k_grouped.append(keep.tile([P, N, PACK], BF16, name=f"k_grouped_{g}", align_bytes=256))
             if g < PASSES - 1:
-                k_codes.append(keep.tile([P, N], U32, name=f"k_codes_{g}", tag=code_tags[g], align_bytes=64))
-            k_scales.append(keep.tile([P, N], U8, name=f"k_scales_{g}", align_bytes=64))
-            q_grouped.append(keep.tile([P, NQ, PACK], BF16, name=f"q_grouped_{g}", align_bytes=64))
-            q_codes.append(keep.tile([P, NQ], U32, name=f"q_codes_{g}", align_bytes=64))
-            q_scales.append(keep.tile([P, NQ], U8, name=f"q_scales_{g}", align_bytes=64))
+                k_codes.append(keep.tile([P, N], U32, name=f"k_codes_{g}", tag=code_tags[g], align_bytes=256))
+            k_scales.append(keep.tile([P, N], U8, name=f"k_scales_{g}", align_bytes=256))
+            q_grouped.append(keep.tile([P, NQ, PACK], BF16, name=f"q_grouped_{g}", align_bytes=256))
+            q_codes.append(keep.tile([P, NQ], U32, name=f"q_codes_{g}", align_bytes=256))
+            q_scales.append(keep.tile([P, NQ], U8, name=f"q_scales_{g}", align_bytes=256))
 
         def gather_wide(g, j):
             nc.vector.tensor_copy(k_wide[g][:, j, :], k_pool[g * PACK + j].indirect(offsets[:]))
@@ -237,9 +237,9 @@ def tile_attend_knn_kernel(tc, qT, kT, vT, vs, offs, out):
             nc.tensor.transpose(v_turned[:, u, :], v_words[:, u * S : (u + 1) * S], ident_f32[:])
         nc.vector.reciprocal(l_inv[:], l_sum[:])
 
-        w_grouped = keep.tile([P, NQ, PACK], BF16, name="w_grouped", align_bytes=64)
-        w_codes = keep.tile([P, NQ], U32, name="w_codes", align_bytes=64)
-        w_scales = keep.tile([P, NQ], U8, name="w_scales", align_bytes=64)
+        w_grouped = keep.tile([P, NQ, PACK], BF16, name="w_grouped", align_bytes=256)
+        w_codes = keep.tile([P, NQ], U32, name="w_codes", align_bytes=256)
+        w_scales = keep.tile([P, NQ], U8, name="w_scales", align_bytes=256)
         QH = NQ // 2
         for h in range(2):
             qs = slice(h * QH, (h + 1) * QH)
@@ -256,12 +256,12 @@ def tile_attend_knn_kernel(tc, qT, kT, vT, vs, offs, out):
                 scales=w_scales[:, qs],
                 in_=w_grouped[:, qs, :].rearrange("p q t -> p (q t)"),
             )
-        v_codes = keep.tile([P, DV], U32, name="v_codes", align_bytes=64)
-        v_scales = keep.tile([P, DV], U8, name="v_scales", align_bytes=64)
+        v_codes = keep.tile([P, DV], U32, name="v_codes", align_bytes=256)
+        v_scales = keep.tile([P, DV], U8, name="v_scales", align_bytes=256)
         EH = DV // 2
         for h in range(2):
             es = slice(h * EH, (h + 1) * EH)
-            v_grouped = keep.tile([P, EH * PACK], BF16, name=f"v_grouped_{h}", align_bytes=64)
+            v_grouped = keep.tile([P, EH * PACK], BF16, name=f"v_grouped_{h}", align_bytes=256)
             nc.scalar.copy(
                 v_grouped[:].bitcast(F32).rearrange("p (e u) -> p e u", u=2),
                 v_turned[:, :, es].rearrange("p u e -> p e u"),
@@ -282,6 +282,6 @@ def tile_attend_knn_kernel(tc, qT, kT, vT, vs, offs, out):
             start=True,
             stop=True,
         )
-        result = keep.tile([P, DV], F32, name="result")
+        result = keep.tile([P, DV], F32, name="result", align_bytes=256)
         nc.vector.tensor_scalar(result[:], y[:], l_inv[:], None, mult)
         nc.sync.dma_start(out[0], result[:])

@@ -27,6 +27,7 @@ FP8X4 = mybir.dt.float8_e4m3fn_x4
 Exp = mybir.ActivationFunctionType.Exp
 Identity = mybir.ActivationFunctionType.Identity
 mult = mybir.AluOpType.mult
+least = mybir.AluOpType.min
 X = mybir.AxisListType.X
 
 
@@ -81,15 +82,17 @@ def tile_attend_knn_kernel(tc, qT, kT, vT, vs, offs, out):
                 )
             nc.scalar.copy(vs_by_run[:, :, PACK * b : PACK * (b + 1)], spread[:].rearrange("p c m -> p m c"))
 
-        score = psum.tile([P, N], F32, name="score", tag="score_bank")
+        score = [psum.tile([P, N // 2], F32, name=f"score_{u}", tag=f"score_bank_{u}") for u in range(2)]
         k_wide = [keep.tile([P, PACK, N], F32, name=f"k_wide_{g}") for g in range(PASSES - 1)]
         code_tags = ["k_pool_1_0", "k_pool_2_1"]
         NH = N // 2
         last_codes = [
-            keep.tile([P, NH], U32, name=f"last_codes_{h}", tag=f"q_raw_{h}", align_bytes=256) for h in range(2)
+            keep.tile([P, NH], U32, name=f"last_codes_{u}", tag=f"q_raw_{2 * u}", align_bytes=256) for u in range(2)
         ]
         last_wide = keep.tile([P, 2, N], F32, name="last_wide")
-        last_grouped = [keep.tile([P, NH, PACK], BF16, name=f"last_grouped_{h}", align_bytes=256) for h in range(2)]
+        last_grouped = keep.tile([P, N, PACK], BF16, name="last_grouped", align_bytes=256)
+        last_dealt = last_grouped[:].rearrange("p (u s e) j -> p s j u e", u=2, e=2)
+        SH = S // 2
         k_grouped = []
         k_codes = []
         k_scales = []
@@ -111,21 +114,18 @@ def tile_attend_knn_kernel(tc, qT, kT, vT, vs, offs, out):
 
         def group_k(g):
             nc.scalar.copy(
-                k_grouped[g][:].rearrange("p (c i) j -> p c j i", i=PACK),
-                k_wide[g][:].rearrange("p j (c i) -> p c j i", i=PACK),
+                k_grouped[g][:].rearrange("p (u s e) j -> p s j u e", u=2, e=2),
+                k_wide[g][:].rearrange("p j (s u e) -> p s j u e", u=2, e=2),
             )
 
         def group_last(h):
             nc.scalar.copy(
-                last_grouped[h][:, :, 0:2].rearrange("p (c i) j -> p c j i", i=PACK),
-                last_wide[:, :, h * NH : (h + 1) * NH].rearrange("p j (c i) -> p c j i", i=PACK),
+                last_dealt[:, h * SH : (h + 1) * SH, 0:2, :, :],
+                last_wide[:, :, h * NH : (h + 1) * NH].rearrange("p j (s u e) -> p s j u e", u=2, e=2),
             )
 
-        def gather_last(j, h):
-            nc.vector.tensor_copy(
-                last_grouped[h][:, :, j],
-                k_pool[2 * PACK + j].indirect(offsets[:, h * NH // 16 : (h + 1) * NH // 16]),
-            )
+        def gather_last(j):
+            nc.vector.tensor_copy(last_dealt[:, :, j, :, :], k_pool[2 * PACK + j].indirect(offsets[:]))
 
         def quantize_k(g, lo, hi):
             nc.vector.quantize_mx(
@@ -138,19 +138,9 @@ def tile_attend_knn_kernel(tc, qT, kT, vT, vs, offs, out):
             nc.vector.quantize_mx(
                 out=last_codes[h][:].bitcast(FP8X4),
                 scales=k_scales[2][:, h * NH : (h + 1) * NH],
-                in_=last_grouped[h][:].rearrange("p i j -> p (i j)"),
+                in_=last_grouped[:, h * NH : (h + 1) * NH, :].rearrange("p i j -> p (i j)"),
             )
 
-        def multiply_last(h):
-            nc.tensor.matmul_mx(
-                out=score[:, h * NH : (h + 1) * NH],
-                lhsT=q_codes[2][:].bitcast(FP8X4),
-                lhsT_scale=q_scales[2][:],
-                rhs=last_codes[h][:].bitcast(FP8X4),
-                rhs_scale=k_scales[2][:, h * NH : (h + 1) * NH],
-                start=False,
-                stop=(h == 1),
-            )
 
         def group_q(g):
             nc.scalar.copy(
@@ -165,21 +155,23 @@ def tile_attend_knn_kernel(tc, qT, kT, vT, vs, offs, out):
                 in_=q_grouped[g][:].rearrange("p q j -> p (q j)"),
             )
 
-        def multiply(g):
+        def multiply(g, u, stop):
+            columns = slice(u * NH, (u + 1) * NH)
+            codes = last_codes[u][:] if g == PASSES - 1 else k_codes[g][:, columns]
             nc.tensor.matmul_mx(
-                out=score[:],
+                out=score[u][:],
                 lhsT=q_codes[g][:].bitcast(FP8X4),
                 lhsT_scale=q_scales[g][:],
-                rhs=k_codes[g][:].bitcast(FP8X4),
-                rhs_scale=k_scales[g][:],
+                rhs=codes.bitcast(FP8X4),
+                rhs_scale=k_scales[g][:, columns],
                 start=(g == 0),
-                stop=False,
+                stop=stop,
             )
 
 
         vs_row = keep.tile([P, N], F32, name="vs_row")
         nc.vector.tensor_copy(vs_row[:], vs_pool[:].indirect(offsets[:]))
-        vs_turned = psum.tile([P, PACK, P], F32, name="vs_turned")
+        vs_turned = psum.tile([P, PACK, P], F32, name="vs_turned", tag="vs_spread_0")
         for t in range(PACK):
             nc.tensor.transpose(vs_turned[:, t, :], vs_row[:, t:N:PACK], ident_f32[:])
         vs_slot = keep.tile([P, PACK], F32, name="vs_slot")
@@ -197,20 +189,21 @@ def tile_attend_knn_kernel(tc, qT, kT, vT, vs, offs, out):
         for h in range(2):
             group_last(h)
         for j in range(2, PACK):
-            for h in range(2):
-                gather_last(j, h)
+            gather_last(j)
         group_q(0)
         quantize_q(0)
-        multiply(0)
+        multiply(0, 0, False)
+        multiply(0, 1, False)
         quantize_last(0)
         group_q(1)
         quantize_q(1)
-        multiply(1)
-        quantize_last(1)
+        multiply(1, 0, False)
         group_q(2)
         quantize_q(2)
-        multiply_last(0)
-        multiply_last(1)
+        multiply(2, 0, True)
+        quantize_last(1)
+        multiply(2, 1, False)
+        multiply(1, 1, True)
 
         neg_m = keep.tile([P, 1], F32, name="neg_m")
         l_part = keep.tile([P, PACK], F32, name="l_part")
@@ -218,10 +211,20 @@ def tile_attend_knn_kernel(tc, qT, kT, vT, vs, offs, out):
         l_sum = keep.tile([P, 1], F32, name="l_sum")
         l_inv = keep.tile([P, 1], F32, name="l_inv")
         prob = keep.tile([P, PACK, S], F32, name="prob")
-        nc.vector.reduce_max(neg_m[:], score[:], axis=X, negate=True)
-        for t in range(PACK):
+        neg_first = keep.tile([P, 1], F32, name="neg_first")
+        neg_score = keep.tile([P, NH], F32, name="neg_score")
+        nc.vector.reduce_max(neg_first[:], score[0][:], axis=X, negate=True)
+        nc.vector.tensor_scalar(neg_score[:], score[1][:], -1.0, neg_first[:], mult, least, accum_out=neg_m[:])
+        quarters = [2, 3, 0, 1]
+        for t in quarters:
+            source, sign = (score[0], 1.0) if t < 2 else (neg_score, -1.0)
             nc.scalar.activation(
-                prob[:, t, :], score[:, t:N:PACK], Exp, bias=neg_m[:], accum_out=l_part[:, t : t + 1]
+                prob[:, t, :],
+                source[:, t % 2 : NH : 2],
+                Exp,
+                bias=neg_m[:],
+                scale=sign,
+                accum_out=l_part[:, t : t + 1],
             )
 
         nc.scalar.activation(l_copy[:], l_part[:], Identity, accum_out=l_sum[:])
@@ -230,9 +233,9 @@ def tile_attend_knn_kernel(tc, qT, kT, vT, vs, offs, out):
         v_words = v_pairs[:].rearrange("p u s e -> p (u s e)").bitcast(F32)
 
         p_turned = psum.tile([P, PACK, NQ], F32, name="p_turned")
-        for t in range(PACK):
+        for t in quarters:
             nc.tensor.transpose(p_turned[:, t, :], prob[:, t, :], ident_f32[:])
-        v_turned = psum.tile([P, 2, DV], F32, name="v_turned", tag="score_bank")
+        v_turned = psum.tile([P, 2, DV], F32, name="v_turned", tag="score_bank_0")
         for u in range(2):
             nc.tensor.transpose(v_turned[:, u, :], v_words[:, u * S : (u + 1) * S], ident_f32[:])
         nc.vector.reciprocal(l_inv[:], l_sum[:])

@@ -275,16 +275,18 @@ def tile_attend_knn_kernel(tc, qT, kT, vT, vs, offs, out):
                 in_=v_grouped[:],
             )
 
-        y = psum.tile([P, DV], F32, name="y")
-        nc.tensor.matmul_mx(
-            out=y[:],
-            lhsT=w_codes[:].bitcast(FP8X4),
-            lhsT_scale=w_scales[:],
-            rhs=v_codes[:].bitcast(FP8X4),
-            rhs_scale=v_scales[:],
-            start=True,
-            stop=True,
-        )
         result = keep.tile([P, DV], F32, name="result", align_bytes=256)
-        nc.vector.tensor_scalar(result[:], y[:], l_inv[:], None, mult)
+        for h in range(2):
+            es = slice(h * EH, (h + 1) * EH)
+            y = psum.tile([P, EH], F32, name=f"y_{h}", tag=f"vs_spread_{1 + h}")
+            nc.tensor.matmul_mx(
+                out=y[:],
+                lhsT=w_codes[:].bitcast(FP8X4),
+                lhsT_scale=w_scales[:],
+                rhs=v_codes[:, es].bitcast(FP8X4),
+                rhs_scale=v_scales[:, es],
+                start=True,
+                stop=True,
+            )
+            nc.vector.tensor_scalar(result[:, es], y[:], l_inv[:], None, mult)
         nc.sync.dma_start(out[0], result[:])

@@ -45,9 +45,9 @@ def tile_attend_knn_kernel(tc, qT, kT, vT, vs, offs, out):
         k_pool = []
         q_raw = []
 
-        def load_k(g, j, count):
+        def load_k(g, j, count, queue):
             tile = keep.tile([P, count, T], F32, name=f"k_pool_{g}_{j}", tag=f"k_pool_{g}_{j}", align_bytes=256)
-            nc.sync.dma_start(tile[:], k_rows[g, :, j : j + count, :])
+            queue.dma_start(tile[:], k_rows[g, :, j : j + count, :])
             k_pool.extend(tile[:, c, :] for c in range(count))
 
         def load_q(g):
@@ -55,14 +55,14 @@ def tile_attend_knn_kernel(tc, qT, kT, vT, vs, offs, out):
             nc.sync.dma_start(tile[:], q_rows[0, g])
             q_raw.append(tile)
 
-        load_k(0, 0, 2)
+        load_k(0, 0, 2, nc.scalar)
         nc.sync.dma_start(offsets[:], offs)
-        nc.scalar.dma_start(vs_runs[:], vs[0].rearrange("(p c) -> p c", c=RUN))
-        load_k(0, 2, 2)
-        load_k(1, 0, 2)
-        load_k(1, 2, 2)
+        nc.sync.dma_start(vs_runs[:], vs[0].rearrange("(p c) -> p c", c=RUN))
+        load_k(0, 2, 2, nc.sync)
+        load_k(1, 0, 2, nc.sync)
+        load_k(1, 2, 2, nc.sync)
         for j in range(PACK):
-            load_k(2, j, 1)
+            load_k(2, j, 1, nc.sync)
         for g in range(PASSES):
             load_q(g)
         v_pool = keep.tile([P, T], F32, name="v_pool", align_bytes=256)
@@ -71,7 +71,7 @@ def tile_attend_knn_kernel(tc, qT, kT, vT, vs, offs, out):
         ident_f32 = keep.tile([P, P], F32, name="ident_f32")
         make_identity(nc, ident_f32[:])
 
-        vs_pool = keep.tile([P, T], F32, name="vs_pool")
+        vs_pool = keep.tile([P, T], F32, name="vs_pool", tag="k_wide_0", align_bytes=256)
         vs_by_run = vs_pool[:].rearrange("p (m c) -> p m c", c=RUN)
         for b in range(RUN // PACK):
             spread = psum.tile([P, PACK, P], F32, name=f"vs_spread_{b}", tag=f"vs_spread_{b}")
@@ -83,13 +83,11 @@ def tile_attend_knn_kernel(tc, qT, kT, vT, vs, offs, out):
             nc.scalar.copy(vs_by_run[:, :, PACK * b : PACK * (b + 1)], spread[:].rearrange("p c m -> p m c"))
 
         score = [psum.tile([P, N // 2], F32, name=f"score_{u}", tag=f"score_bank_{u}") for u in range(2)]
-        k_wide = [keep.tile([P, PACK, N], F32, name=f"k_wide_{g}") for g in range(PASSES - 1)]
         code_tags = ["k_pool_1_0", "k_pool_2_1"]
         NH = N // 2
         last_codes = [
             keep.tile([P, NH], U32, name=f"last_codes_{u}", tag=f"q_raw_{2 * u}", align_bytes=256) for u in range(2)
         ]
-        last_wide = keep.tile([P, 2, N], F32, name="last_wide")
         last_grouped = keep.tile([P, N, PACK], BF16, name="last_grouped", align_bytes=256)
         last_dealt = last_grouped[:].rearrange("p (u s e) j -> p s j u e", u=2, e=2)
         SH = S // 2
@@ -177,6 +175,12 @@ def tile_attend_knn_kernel(tc, qT, kT, vT, vs, offs, out):
         vs_slot = keep.tile([P, PACK], F32, name="vs_slot")
         nc.scalar.copy(vs_slot[:], vs_turned[:, :, 0])
 
+        wide_tags = ["k_wide_0", "k_pool_0_2"]
+        k_wide = [
+            keep.tile([P, PACK, N], F32, name=f"k_wide_{g}", tag=wide_tags[g], align_bytes=256)
+            for g in range(PASSES - 1)
+        ]
+        last_wide = keep.tile([P, 2, N], F32, name="last_wide", tag="k_pool_1_2", align_bytes=256)
         for g in range(PASSES - 1):
             for j in range(PACK):
                 gather_wide(g, j)

@@ -14,6 +14,7 @@ K_PASS = P * PACK
 PASSES = D // K_PASS
 S = N // PACK
 RUN = T // P
+SHARE = 64
 
 FLOPS = 2 * NQ * N * D + 2 * NQ * N * DV
 BYTES = 4 * (D * T + DV * T + T + D * NQ + NQ * DV) + 2 * P * (N // 16)
@@ -24,6 +25,7 @@ U32 = mybir.dt.uint32
 U16 = mybir.dt.uint16
 U8 = mybir.dt.uint8
 FP8X4 = mybir.dt.float8_e4m3fn_x4
+Copy = mybir.ActivationFunctionType.Copy
 Exp = mybir.ActivationFunctionType.Exp
 Identity = mybir.ActivationFunctionType.Identity
 mult = mybir.AluOpType.mult
@@ -123,7 +125,10 @@ def tile_attend_knn_kernel(tc, qT, kT, vT, vs, offs, out):
             )
 
         def gather_last(j):
-            nc.vector.tensor_copy(last_dealt[:, :, j, :, :], k_pool[2 * PACK + j].indirect(offsets[:]))
+            cut = N - SHARE
+            window = k_pool[2 * PACK + j]
+            nc.vector.tensor_copy(last_dealt[:, : cut // PACK, j], window.indirect(offsets[:, : cut // 16]))
+            nc.scalar.activation(last_dealt[:, cut // PACK :, j], window.indirect(offsets[:, cut // 16 :]), Copy)
 
         def quantize_k(g, lo, hi):
             nc.vector.quantize_mx(

@@ -15,6 +15,7 @@ PASSES = D // K_PASS
 S = N // PACK
 RUN = T // P
 SHARE = 64
+V_SHARE = 64
 
 FLOPS = 2 * NQ * N * D + 2 * NQ * N * DV
 BYTES = 4 * (D * T + DV * T + T + D * NQ + NQ * DV) + 2 * P * (N // 16)
@@ -215,8 +216,7 @@ def tile_attend_knn_kernel(tc, qT, kT, vT, vs, offs, out):
         multiply(1, 1, True)
 
         neg_m = keep.tile([P, 1], F32, name="neg_m")
-        l_part = keep.tile([P, PACK], F32, name="l_part")
-        l_copy = keep.tile([P, PACK], F32, name="l_copy")
+        p_again = keep.tile([P, PACK, S], F32, name="p_again")
         l_sum = keep.tile([P, 1], F32, name="l_sum")
         l_inv = keep.tile([P, 1], F32, name="l_inv")
         prob = keep.tile([P, PACK, S], F32, name="prob")
@@ -225,20 +225,24 @@ def tile_attend_knn_kernel(tc, qT, kT, vT, vs, offs, out):
         nc.vector.reduce_max(neg_first[:], score[0][:], axis=X, negate=True)
         nc.vector.tensor_scalar(neg_score[:], score[1][:], -1.0, neg_first[:], mult, least, accum_out=neg_m[:])
         quarters = [2, 3, 0, 1]
-        for t in quarters:
-            source, sign = (score[0], 1.0) if t < 2 else (neg_score, -1.0)
+        nc.scalar.activation(
+            prob[:, 2:PACK, :],
+            neg_score[:].rearrange("p (s e) -> p e s", e=2),
+            Exp,
+            bias=neg_m[:],
+            scale=-1.0,
+        )
+        for t in range(2):
             nc.scalar.activation(
-                prob[:, t, :],
-                source[:, t % 2 : NH : 2],
-                Exp,
-                bias=neg_m[:],
-                scale=sign,
-                accum_out=l_part[:, t : t + 1],
+                prob[:, t, :], score[0][:, t:NH:2], Exp, bias=neg_m[:]
             )
 
-        nc.scalar.activation(l_copy[:], l_part[:], Identity, accum_out=l_sum[:])
         v_pairs = keep.tile([P, 2, S, 2], BF16, name="v_pairs")
-        nc.vector.tensor_copy(v_pairs[:].rearrange("p u s e -> p s u e"), v_pool[:].indirect(offsets[:]))
+        v_dealt = v_pairs[:].rearrange("p u s e -> p s u e")
+        v_cut = N - V_SHARE
+        nc.vector.tensor_copy(v_dealt[:, : v_cut // PACK], v_pool[:].indirect(offsets[:, : v_cut // 16]))
+        nc.scalar.activation(v_dealt[:, v_cut // PACK :], v_pool[:].indirect(offsets[:, v_cut // 16 :]), Copy)
+        nc.scalar.activation(p_again[:], prob[:], Identity, accum_out=l_sum[:])
         v_words = v_pairs[:].rearrange("p u s e -> p (u s e)").bitcast(F32)
 
         p_turned = psum.tile([P, PACK, NQ], F32, name="p_turned")
@@ -247,7 +251,6 @@ def tile_attend_knn_kernel(tc, qT, kT, vT, vs, offs, out):
         v_turned = psum.tile([P, 2, DV], F32, name="v_turned", tag="score_bank_0")
         for u in range(2):
             nc.tensor.transpose(v_turned[:, u, :], v_words[:, u * S : (u + 1) * S], ident_f32[:])
-        nc.vector.reciprocal(l_inv[:], l_sum[:])
 
         w_grouped = keep.tile([P, NQ, PACK], BF16, name="w_grouped", align_bytes=256)
         w_codes = keep.tile([P, NQ], U32, name="w_codes", align_bytes=256)
@@ -284,6 +287,7 @@ def tile_attend_knn_kernel(tc, qT, kT, vT, vs, offs, out):
                 in_=v_grouped[:],
             )
 
+        nc.vector.reciprocal(l_inv[:], l_sum[:])
         result = keep.tile([P, DV], F32, name="result", align_bytes=256)
         for h in range(2):
             es = slice(h * EH, (h + 1) * EH)

from contextlib import ExitStack

import concourse.mybir as mybir
from concourse.masks import make_identity

P = 128
D = 1536
T = 2048
N = 512
NQ = 128
DV = 128
PACK = 4
K_PASS = P * PACK
PASSES = D // K_PASS
S = N // PACK
RUN = T // P
SHARE = 64
V_SHARE = 64

FLOPS = 2 * NQ * N * D + 2 * NQ * N * DV
BYTES = 4 * (D * T + DV * T + T + D * NQ + NQ * DV) + 2 * P * (N // 16)

F32 = mybir.dt.float32
BF16 = mybir.dt.bfloat16
U32 = mybir.dt.uint32
U16 = mybir.dt.uint16
U8 = mybir.dt.uint8
FP8X4 = mybir.dt.float8_e4m3fn_x4
Copy = mybir.ActivationFunctionType.Copy
Exp = mybir.ActivationFunctionType.Exp
Identity = mybir.ActivationFunctionType.Identity
mult = mybir.AluOpType.mult
least = mybir.AluOpType.min
X = mybir.AxisListType.X


def tile_attend_knn_kernel(tc, qT, kT, vT, vs, offs, out):
    nc = tc.nc
    with ExitStack() as ctx:
        keep = ctx.enter_context(tc.tile_pool(name="keep", bufs=1))
        psum = ctx.enter_context(tc.psum_pool(name="psum", bufs=1))

        offsets = keep.tile([P, N // 16], U16, name="offsets", align_bytes=256)
        vs_runs = keep.tile([P, RUN], F32, name="vs_runs", align_bytes=256)

        k_rows = kT.rearrange("(g p j) w -> g p j w", p=P, j=PACK)
        q_rows = qT.rearrange("b (g p j) w -> b g p j w", p=P, j=PACK)
        k_pool = []
        q_raw = []

        def load_k(g, j, count, queue):
            tile = keep.tile([P, count, T], F32, name=f"k_pool_{g}_{j}", tag=f"k_pool_{g}_{j}", align_bytes=256)
            queue.dma_start(tile[:], k_rows[g, :, j : j + count, :])
            k_pool.extend(tile[:, c, :] for c in range(count))

        def load_q(g):
            tile = keep.tile([P, PACK, NQ], F32, name=f"q_raw_{g}", tag=f"q_raw_{g}", align_bytes=256)
            nc.sync.dma_start(tile[:], q_rows[0, g])
            q_raw.append(tile)

        load_k(0, 0, 2, nc.scalar)
        nc.sync.dma_start(offsets[:], offs)
        nc.sync.dma_start(vs_runs[:], vs[0].rearrange("(p c) -> p c", c=RUN))
        load_k(0, 2, 2, nc.sync)
        load_k(1, 0, 2, nc.sync)
        load_k(1, 2, 2, nc.sync)
        for j in range(PACK):
            load_k(2, j, 1, nc.sync)
        for g in range(PASSES):
            load_q(g)
        v_pool = keep.tile([P, T], F32, name="v_pool", align_bytes=256)
        nc.sync.dma_start(v_pool[:], vT)

        ident_f32 = keep.tile([P, P], F32, name="ident_f32")
        make_identity(nc, ident_f32[:])

        vs_pool = keep.tile([P, T], F32, name="vs_pool", tag="k_wide_0", align_bytes=256)
        vs_by_run = vs_pool[:].rearrange("p (m c) -> p m c", c=RUN)
        for b in range(RUN // PACK):
            spread = psum.tile([P, PACK, P], F32, name=f"vs_spread_{b}", tag=f"vs_spread_{b}")
            for c in range(PACK):
                column = PACK * b + c
                nc.tensor.transpose(
                    spread[:, c, :], vs_runs[:, column : column + 1].to_broadcast([P, P]), ident_f32[:]
                )
            nc.scalar.copy(vs_by_run[:, :, PACK * b : PACK * (b + 1)], spread[:].rearrange("p c m -> p m c"))

        score = [psum.tile([P, N // 2], F32, name=f"score_{u}", tag=f"score_bank_{u}") for u in range(2)]
        code_tags = ["k_pool_1_0", "k_pool_2_1"]
        NH = N // 2
        last_codes = [
            keep.tile([P, NH], U32, name=f"last_codes_{u}", tag=f"q_raw_{2 * u}", align_bytes=256) for u in range(2)
        ]
        last_grouped = keep.tile([P, N, PACK], BF16, name="last_grouped", align_bytes=256)
        last_dealt = last_grouped[:].rearrange("p (u s e) j -> p s j u e", u=2, e=2)
        SH = S // 2
        k_grouped = []
        k_codes = []
        k_scales = []
        q_grouped = []
        q_codes = []
        q_scales = []
        for g in range(PASSES):
            if g < PASSES - 1:
                k_grouped.append(keep.tile([P, N, PACK], BF16, name=f"k_grouped_{g}", align_bytes=256))
            if g < PASSES - 1:
                k_codes.append(keep.tile([P, N], U32, name=f"k_codes_{g}", tag=code_tags[g], align_bytes=256))
            k_scales.append(keep.tile([P, N], U8, name=f"k_scales_{g}", align_bytes=256))
            q_grouped.append(keep.tile([P, NQ, PACK], BF16, name=f"q_grouped_{g}", align_bytes=256))
            q_codes.append(keep.tile([P, NQ], U32, name=f"q_codes_{g}", align_bytes=256))
            q_scales.append(keep.tile([P, NQ], U8, name=f"q_scales_{g}", align_bytes=256))

        def gather_wide(g, j):
            nc.vector.tensor_copy(k_wide[g][:, j, :], k_pool[g * PACK + j].indirect(offsets[:]))

        def group_k(g):
            nc.scalar.copy(
                k_grouped[g][:].rearrange("p (u s e) j -> p s j u e", u=2, e=2),
                k_wide[g][:].rearrange("p j (s u e) -> p s j u e", u=2, e=2),
            )

        def group_last(h):
            nc.scalar.copy(
                last_dealt[:, h * SH : (h + 1) * SH, 0:2, :, :],
                last_wide[:, :, h * NH : (h + 1) * NH].rearrange("p j (s u e) -> p s j u e", u=2, e=2),
            )

        def gather_last(j):
            cut = N - SHARE
            window = k_pool[2 * PACK + j]
            nc.vector.tensor_copy(last_dealt[:, : cut // PACK, j], window.indirect(offsets[:, : cut // 16]))
            nc.scalar.activation(last_dealt[:, cut // PACK :, j], window.indirect(offsets[:, cut // 16 :]), Copy)

        def quantize_k(g, lo, hi):
            nc.vector.quantize_mx(
                out=k_codes[g][:, lo:hi].bitcast(FP8X4),
                scales=k_scales[g][:, lo:hi],
                in_=k_grouped[g][:, lo:hi, :].rearrange("p i j -> p (i j)"),
            )

        def quantize_last(h):
            nc.vector.quantize_mx(
                out=last_codes[h][:].bitcast(FP8X4),
                scales=k_scales[2][:, h * NH : (h + 1) * NH],
                in_=last_grouped[:, h * NH : (h + 1) * NH, :].rearrange("p i j -> p (i j)"),
            )


        def group_q(g):
            nc.scalar.copy(
                q_grouped[g][:].rearrange("p (c i) j -> p c j i", i=PACK),
                q_raw[g][:].rearrange("p j (c i) -> p c j i", i=PACK),
            )

        def quantize_q(g):
            nc.vector.quantize_mx(
                out=q_codes[g][:].bitcast(FP8X4),
                scales=q_scales[g][:],
                in_=q_grouped[g][:].rearrange("p q j -> p (q j)"),
            )

        def multiply(g, u, stop):
            columns = slice(u * NH, (u + 1) * NH)
            codes = last_codes[u][:] if g == PASSES - 1 else k_codes[g][:, columns]
            nc.tensor.matmul_mx(
                out=score[u][:],
                lhsT=q_codes[g][:].bitcast(FP8X4),
                lhsT_scale=q_scales[g][:],
                rhs=codes.bitcast(FP8X4),
                rhs_scale=k_scales[g][:, columns],
                start=(g == 0),
                stop=stop,
            )


        vs_row = keep.tile([P, N], F32, name="vs_row")
        nc.vector.tensor_copy(vs_row[:], vs_pool[:].indirect(offsets[:]))
        vs_turned = psum.tile([P, PACK, P], F32, name="vs_turned", tag="vs_spread_0")
        for t in range(PACK):
            nc.tensor.transpose(vs_turned[:, t, :], vs_row[:, t:N:PACK], ident_f32[:])
        vs_slot = keep.tile([P, PACK], F32, name="vs_slot")
        nc.scalar.copy(vs_slot[:], vs_turned[:, :, 0])

        wide_tags = ["k_wide_0", "k_pool_0_2"]
        k_wide = [
            keep.tile([P, PACK, N], F32, name=f"k_wide_{g}", tag=wide_tags[g], align_bytes=256)
            for g in range(PASSES - 1)
        ]
        last_wide = keep.tile([P, 2, N], F32, name="last_wide", tag="k_pool_1_2", align_bytes=256)
        for g in range(PASSES - 1):
            for j in range(PACK):
                gather_wide(g, j)
                if g > 0 and j == 1:
                    quantize_k(g - 1, 0, N)
            group_k(g)
        for j in range(2):
            nc.vector.tensor_copy(last_wide[:, j, :], k_pool[2 * PACK + j].indirect(offsets[:]))
        quantize_k(1, 0, N)
        for h in range(2):
            group_last(h)
        for j in range(2, PACK):
            gather_last(j)
        group_q(0)
        quantize_q(0)
        multiply(0, 0, False)
        multiply(0, 1, False)
        quantize_last(0)
        group_q(1)
        quantize_q(1)
        multiply(1, 0, False)
        group_q(2)
        quantize_q(2)
        multiply(2, 0, True)
        quantize_last(1)
        multiply(2, 1, False)
        multiply(1, 1, True)

        neg_m = keep.tile([P, 1], F32, name="neg_m")
        p_again = keep.tile([P, PACK, S], F32, name="p_again")
        l_sum = keep.tile([P, 1], F32, name="l_sum")
        l_inv = keep.tile([P, 1], F32, name="l_inv")
        prob = keep.tile([P, PACK, S], F32, name="prob")
        neg_first = keep.tile([P, 1], F32, name="neg_first")
        neg_score = keep.tile([P, NH], F32, name="neg_score")
        nc.vector.reduce_max(neg_first[:], score[0][:], axis=X, negate=True)
        nc.vector.tensor_scalar(neg_score[:], score[1][:], -1.0, neg_first[:], mult, least, accum_out=neg_m[:])
        quarters = [2, 3, 0, 1]
        nc.scalar.activation(
            prob[:, 2:PACK, :],
            neg_score[:].rearrange("p (s e) -> p e s", e=2),
            Exp,
            bias=neg_m[:],
            scale=-1.0,
        )
        for t in range(2):
            nc.scalar.activation(
                prob[:, t, :], score[0][:, t:NH:2], Exp, bias=neg_m[:]
            )

        v_pairs = keep.tile([P, 2, S, 2], BF16, name="v_pairs")
        v_dealt = v_pairs[:].rearrange("p u s e -> p s u e")
        v_cut = N - V_SHARE
        nc.vector.tensor_copy(v_dealt[:, : v_cut // PACK], v_pool[:].indirect(offsets[:, : v_cut // 16]))
        nc.scalar.activation(v_dealt[:, v_cut // PACK :], v_pool[:].indirect(offsets[:, v_cut // 16 :]), Copy)
        nc.scalar.activation(p_again[:], prob[:], Identity, accum_out=l_sum[:])
        v_words = v_pairs[:].rearrange("p u s e -> p (u s e)").bitcast(F32)

        p_turned = psum.tile([P, PACK, NQ], F32, name="p_turned")
        for t in quarters:
            nc.tensor.transpose(p_turned[:, t, :], prob[:, t, :], ident_f32[:])
        v_turned = psum.tile([P, 2, DV], F32, name="v_turned", tag="score_bank_0")
        for u in range(2):
            nc.tensor.transpose(v_turned[:, u, :], v_words[:, u * S : (u + 1) * S], ident_f32[:])

        w_grouped = keep.tile([P, NQ, PACK], BF16, name="w_grouped", align_bytes=256)
        w_codes = keep.tile([P, NQ], U32, name="w_codes", align_bytes=256)
        w_scales = keep.tile([P, NQ], U8, name="w_scales", align_bytes=256)
        QH = NQ // 2
        for h in range(2):
            qs = slice(h * QH, (h + 1) * QH)
            nc.vector.tensor_tensor(
                w_grouped[:, qs, :],
                p_turned[:, :, qs].rearrange("p t q -> p q t"),
                vs_slot[:].unsqueeze(1).to_broadcast([P, QH, PACK]),
                mult,
            )
        for h in range(2):
            qs = slice(h * QH, (h + 1) * QH)
            nc.vector.quantize_mx(
                out=w_codes[:, qs].bitcast(FP8X4),
                scales=w_scales[:, qs],
                in_=w_grouped[:, qs, :].rearrange("p q t -> p (q t)"),
            )
        v_codes = keep.tile([P, DV], U32, name="v_codes", align_bytes=256)
        v_scales = keep.tile([P, DV], U8, name="v_scales", align_bytes=256)
        EH = DV // 2
        for h in range(2):
            es = slice(h * EH, (h + 1) * EH)
            v_grouped = keep.tile([P, EH * PACK], BF16, name=f"v_grouped_{h}", align_bytes=256)
            nc.scalar.copy(
                v_grouped[:].bitcast(F32).rearrange("p (e u) -> p e u", u=2),
                v_turned[:, :, es].rearrange("p u e -> p e u"),
            )
            nc.vector.quantize_mx(
                out=v_codes[:, es].bitcast(FP8X4),
                scales=v_scales[:, es],
                in_=v_grouped[:],
            )

        nc.vector.reciprocal(l_inv[:], l_sum[:])
        result = keep.tile([P, DV], F32, name="result", align_bytes=256)
        for h in range(2):
            es = slice(h * EH, (h + 1) * EH)
            y = psum.tile([P, EH], F32, name=f"y_{h}", tag=f"vs_spread_{1 + h}")
            nc.tensor.matmul_mx(
                out=y[:],
                lhsT=w_codes[:].bitcast(FP8X4),
                lhsT_scale=w_scales[:],
                rhs=v_codes[:, es].bitcast(FP8X4),
                rhs_scale=v_scales[:, es],
                start=True,
                stop=True,
            )
            nc.vector.tensor_scalar(result[:, es], y[:], l_inv[:], None, mult)
        nc.sync.dma_start(out[0], result[:])
